import numpy as np
import ml_dtypes


def mxq(x, axis, fmt="e4m3"):
    dtype, down = {"e4m3": (ml_dtypes.float8_e4m3fn, 7), "e5m2": (ml_dtypes.float8_e5m2, 14)}[fmt]
    v = np.moveaxis(np.asarray(x, np.float32).astype(ml_dtypes.bfloat16).astype(np.float64), axis, -1)
    blocks = v.reshape(v.shape[:-1] + (-1, 32))
    amax = np.abs(blocks).max(-1, keepdims=True)
    byte = np.maximum(np.where(amax > 0, np.frexp(amax)[1] - 1 + 127, 0) - down, 1)
    scale = np.exp2(byte - 127.0)
    codes = (blocks / scale).astype(np.float32).astype(dtype).astype(np.float64)
    return np.moveaxis((codes * scale).reshape(v.shape), -1, axis)


WIDE = False


def mx_kscale(k):
    if not WIDE:
        return np.ones(k)
    levels = np.array([10, -10, 5, -5, 0])
    if k % 512:
        return np.exp2(np.random.permutation(np.resize(levels, k // 32))).repeat(32)
    a = np.empty((k // 512, 16))
    for p in range(k // 512):
        a[p, :8] = np.random.permutation(np.resize(levels, 8))
        for g in range(8):
            far = levels[np.abs(levels - a[p, g]) >= 10]
            a[p, g + 8] = far[np.random.randint(len(far))]
    return np.exp2(a.ravel()).repeat(32)


def f64(x):
    return np.asarray(x).astype(np.float64)


def striped(idx):
    return np.tile(np.asarray(idx).reshape(-1, 16).T, (8, 1)).astype(np.uint16)


def unstriped(offs):
    return offs[:16].T.reshape(-1).astype(np.int64)


E2M1 = np.array([0.0, 0.5, 1.0, 1.5, 2.0, 3.0, 4.0, 6.0, -0.0, -0.5, -1.0, -1.5, -2.0, -3.0, -4.0, -6.0])


def pack_weight(w, fmt):
    k, n = w.shape
    w = f64(np.asarray(w, np.float32).astype(ml_dtypes.bfloat16)).reshape(k // 32, 32, n)
    amax = np.abs(w).max(1)
    if fmt == "e4m3":
        byte = np.frexp(amax)[1] - 1 + 127 - 7
    else:
        mant, ex = np.frexp(amax / 6.0)
        byte = np.where(mant > 0.5, ex, ex - 1) + 127
    byte = np.clip(np.where(amax > 0, byte, 1), 1, 254)
    scaled = (w * np.exp2(127.0 - byte)[:, None, :]).reshape(k, n).astype(np.float32)
    by_word = np.ascontiguousarray(scaled.reshape(k // 512, 128, 4, n).transpose(0, 1, 3, 2))
    if fmt == "e4m3":
        words = by_word.astype(ml_dtypes.float8_e4m3fn).view(np.uint8)
    else:
        c = by_word.astype(ml_dtypes.float4_e2m1fn).view(np.uint8) & 0xF
        words = (c[..., 0::2] | (c[..., 1::2] << 4)).reshape(k // 512, 128, 2 * n)
    return np.ascontiguousarray(words), np.ascontiguousarray(byte.astype(np.uint8).reshape(k // 512, 16, n))


def unpack_weight(words, scales, fmt):
    g, _, n = scales.shape
    words = np.ascontiguousarray(words).reshape(g, 128, n, -1)
    if fmt == "e4m3":
        vals = words.view(ml_dtypes.float8_e4m3fn).astype(np.float64)
    else:
        nib = np.empty((g, 128, n, 4), np.uint8)
        nib[..., 0::2] = words & 0xF
        nib[..., 1::2] = words >> 4
        vals = E2M1[nib]
    vals = vals * np.repeat(np.exp2(scales.astype(np.float64) - 127.0), 8, axis=1)[..., None]
    return vals.transpose(0, 1, 3, 2).reshape(g * 512, n)


def softplus(v):
    return np.log(1.0 + np.exp(v))


def sigmoid(v):
    return 1.0 / (1.0 + np.exp(-v))


D, K, R, T, I, Q, G = 512, 512, 512, 2048, 512, 128, 64


def setup_inputs():
    n = np.random.standard_normal
    idx = np.random.permutation(T)[:I]
    fd = mx_kscale(D)
    fk = mx_kscale(K)
    fr = mx_kscale(R)
    keysp = pack_weight(n((D, T)) / fd[:, None], "e4m3")
    tabp = pack_weight(n((K, T)) / fk[:, None], "e4m3")
    return {
        "query": (n((D, Q)) * 0.9 / np.sqrt(D) * fd[:, None]).astype(np.float32),
        "keys_words": keysp[0],
        "keys_scales": keysp[1],
        "th": (np.random.uniform(-0.3, 0.6, (Q, 1))).astype(np.float32),
        "reserve": (np.random.uniform(50.0, 200.0, (Q, 1))).astype(np.float32),
        "tab_words": tabp[0],
        "tab_scales": tabp[1],
        "w1": (n((K, R)) * 1 / np.sqrt(K) * fk[:, None]).astype(np.float32),
        "temper": (np.random.uniform(0.4, 1.0, (R, 1))).astype(np.float32),
        "gout": (n((R, Q)) * 1 / np.sqrt(R) * fr[:, None]).astype(np.float32),
        "hsc": (np.random.uniform(0.7, 1.4, (R, 1)) / fr[:, None]).astype(np.float32),
        "old": (0.5 * n((Q, T))).astype(np.float32),
        "offs": striped(idx),
    }


def reference(query, keys_words, keys_scales, th, reserve, tab_words, tab_scales, w1, temper, gout, hsc, old, offs):
    idx = unstriped(offs)
    keysu = unpack_weight(keys_words, keys_scales, "e4m3")
    tabu = unpack_weight(tab_words, tab_scales, "e4m3")
    queryq = mxq(f64(query), 0, "e4m3")
    keysidxg = keysu[:, idx]
    a = queryq.T @ keysidxg
    p = softplus(a - f64(th))
    z = np.sum(p, axis=1, keepdims=True) + f64(reserve)
    w1q = mxq(f64(w1), 0, "e4m3")
    tabidxg = tabu[:, idx]
    zh = w1q.T @ tabidxg
    ht = np.exp(zh * f64(temper))
    mz = ht.reshape(R, G, I // G).sum(axis=2)
    mzr = np.repeat(mz, I // G, axis=1)
    hv = ht / mzr * 4.0
    hs1 = hv * f64(hsc)
    goutq = mxq(f64(gout), 0, "e4m3")
    hs1q = mxq(hs1, 0, "e4m3")
    c0 = goutq.T @ hs1q
    dz = np.sum(c0 * p / np.square(z) * (-1.0), axis=1, keepdims=True)
    dp = c0 / z + dz
    da = dp * sigmoid(a - f64(th))
    gs = da * 512.0
    gf = np.zeros((Q, T))
    gf[:, idx] = gs
    y = f64(old) + gf
    return y

@@ -1,0 +1,210 @@
+from contextlib import ExitStack
+
+import concourse.mybir as mybir
+from concourse.masks import make_identity
+
+F32 = mybir.dt.float32
+BF16 = mybir.dt.bfloat16
+I32 = mybir.dt.int32
+U32 = mybir.dt.uint32
+U16 = mybir.dt.uint16
+U8 = mybir.dt.uint8
+FP8X4 = mybir.dt.float8_e4m3fn_x4
+ALU = mybir.AluOpType
+ACT = mybir.ActivationFunctionType
+
+P = 128
+PACK = 4
+T = 2048
+SLOTS = 512
+Q = 128
+R = 512
+GROUP = 8
+HALVES = 2
+HALF = SLOTS // HALVES
+RUN = 4
+RUNS = HALF // GROUP // RUN
+OUT_CHUNKS = 4
+CAP = 32.0
+FLOPS = 2 * 512 * SLOTS * (Q + R + Q)
+
+
+def tile_attend_blrshared_capped_kernel(tc, query, keys_words, keys_scales, th, reserve, tab_words, tab_scales,
+                                         w1, temper, gout, hsc, old, offs, out):
+    nc = tc.nc
+    with ExitStack() as ctx:
+        sb = ctx.enter_context(tc.tile_pool(name="sb", bufs=1))
+        ps = ctx.enter_context(tc.psum_pool(name="ps", bufs=1))
+
+        def tile(name, shape, dtype, tag=None):
+            return sb.tile(shape, dtype, name=name, tag=tag or name, align_bytes=64)
+
+        def load_words(name, words, tag):
+            pool_words = tile(name, [P, T], U32, tag)
+            nc.sync.dma_start(out=pool_words[:].bitcast(I32), in_=words[0].rearrange("p n t -> p (n t)").bitcast(I32))
+            return pool_words
+
+        def load_scales(pool_scales, scales, queue):
+            for quad in range(4):
+                queue.dma_start(out=pool_scales[32 * quad : 32 * quad + 4, :].bitcast(I32),
+                                    in_=scales[0, 4 * quad : 4 * quad + 4, :].bitcast(I32))
+
+        def load_column(name, vec, width, queue):
+            col = tile(name, [P, width], F32)
+            queue.dma_start(out=col[:], in_=vec.rearrange("(p t) o -> p (t o)", t=width))
+            return col
+
+        def load_rows(name, mat, width, tag):
+            raw = tile(name, [P, PACK, width], F32, tag)
+            nc.sync.dma_start(out=raw[:], in_=mat.rearrange("(p j) c -> p j c", j=PACK))
+            return raw
+
+        def quantize(name, grouped, width):
+            codes = tile(name + "_codes", [P, width], U32)
+            scales = tile(name + "_scales", [P, width], U8)
+            nc.vector.quantize_mx(out=codes[:].bitcast(FP8X4), scales=scales[:], in_=grouped)
+            return codes, scales
+
+        def gather(name, window, offsets, width, dtype):
+            picked = tile(name, [P, width], dtype)
+            nc.vector.tensor_copy(out=picked[:], in_=window[:].indirect(offsets))
+            return picked
+
+        def mx_product(acc, lhs_codes, lhs_scales, rhs_codes, rhs_scales):
+            nc.tensor.matmul_mx(out=acc, lhsT=lhs_codes.bitcast(FP8X4), lhsT_scale=lhs_scales,
+                                rhs=rhs_codes.bitcast(FP8X4), rhs_scale=rhs_scales, start=True, stop=True)
+
+        def interleave_rows(name, raw):
+            grouped = tile(name, [P, Q, PACK], BF16)
+            nc.vector.tensor_copy(out=grouped[:].rearrange("p (c i) j -> p c j i", i=4),
+                                  in_=raw[:].rearrange("p j (c i) -> p c j i", i=4))
+            return grouped[:].rearrange("p q j -> p (q j)")
+
+        offsets = sb.tile([P, SLOTS // 16], U16, name="offsets")
+        nc.sync.dma_start(offsets[:], offs)
+        tab_pool_scales = tile("tab_pool_scales", [P, T], U8)
+        keys_pool_scales = tile("keys_pool_scales", [P, T], U8)
+        nc.vector.memset(tab_pool_scales[:].bitcast(I32), 0)
+        nc.vector.memset(keys_pool_scales[:].bitcast(I32), 0)
+        load_scales(tab_pool_scales, tab_scales, nc.scalar)
+        w_raw = load_rows("w_raw", w1, R, "big0")
+        tab_pool = load_words("tab_pool", tab_words, "big1")
+        temper_sb = load_column("temper_sb", temper, PACK, nc.gpsimd)
+        th_sb = load_column("th_sb", th, 1, nc.gpsimd)
+        hsc_sb = load_column("hsc_sb", hsc, PACK, nc.gpsimd)
+        reserve_sb = load_column("reserve_sb", reserve, 1, nc.gpsimd)
+        q_raw = load_rows("q_raw", query, Q, "rows")
+        load_scales(keys_pool_scales, keys_scales, nc.sync)
+
+        ident = tile("ident", [P, P], F32)
+        make_identity(nc, ident[:])
+        scattered = tile("scattered", [P, T], F32)
+        nc.vector.memset(scattered[:], 0.0)
+
+        neg_th = tile("neg_th", [P, 1], F32)
+        nc.scalar.activation(out=neg_th[:], in_=th_sb[:], func=ACT.Identity, scale=-1.0)
+        th_cap = tile("th_cap", [P, 1], F32)
+        nc.scalar.activation(out=th_cap[:], in_=th_sb[:], func=ACT.Identity, bias=CAP)
+        hsc4 = tile("hsc4", [P, RUNS, PACK, RUN], F32)
+        nc.scalar.activation(out=hsc4[:], in_=hsc_sb[:].unsqueeze(1).unsqueeze(3).to_broadcast([P, RUNS, PACK, RUN]),
+                             func=ACT.Identity, scale=4.0)
+
+        tab_scales_g = gather("tab_scales_g", tab_pool_scales, offsets[:], SLOTS, U8)
+        w_grouped = tile("w_grouped", [P, PACK, P, PACK], BF16)
+        nc.vector.tensor_copy(out=w_grouped[:].rearrange("p t m j -> p m j t"),
+                              in_=w_raw[:].rearrange("p j (m t) -> p m j t", t=PACK))
+        keys_pool = load_words("keys_pool", keys_words, "big0")
+        w_codes, w_scales = quantize("w", w_grouped[:].rearrange("p t m j -> p (t m j)"), R)
+
+        cols = HALF // 16
+        ht = []
+        for h in range(HALVES):
+            tab_g = gather(f"tab_g{h}", tab_pool, offsets[:, h * cols : (h + 1) * cols], HALF, U32)
+            ht.append(tile(f"ht{h}", [P, GROUP, RUNS, PACK, RUN], F32))
+            for pair in range(2):
+                zh = ps.tile([P, 2, HALF], F32, name=f"zh{h}{pair}")
+                for u in range(2):
+                    t = 2 * pair + u
+                    mx_product(zh[:, u, :], w_codes[:, t * P : (t + 1) * P], w_scales[:, t * P : (t + 1) * P],
+                               tab_g[:], tab_scales_g[:, h * HALF : (h + 1) * HALF])
+                for u in range(2):
+                    t = 2 * pair + u
+                    nc.scalar.activation(out=ht[h][:, :, :, t, :],
+                                         in_=zh[:, u, :].rearrange("p (b i j) -> p j b i", i=RUN, j=GROUP),
+                                         func=ACT.Exp, scale=temper_sb[:, t : t + 1])
+
+        sums = []
+        for h in range(HALVES):
+            turn = ps.tile([P, 2, P], F32, name=f"turn{h}")
+            for j in range(GROUP):
+                nc.tensor.matmul(out=turn[:, 0, :], lhsT=ht[h][:, j].rearrange("p b t i -> p (b t i)"), rhs=ident[:],
+                                 is_transpose=True, start=(j == 0), stop=(j == GROUP - 1))
+            sums.append(turn)
+
+        q_codes, q_scales = quantize("q", interleave_rows("q_grouped", q_raw), Q)
+        g_raw = load_rows("g_raw", gout, Q, "rows")
+        old_sb = tile("old_sb", [P, T], F32, "big1")
+        nc.sync.dma_start(out=old_sb[:], in_=old)
+        keys_scales_g = gather("keys_scales_g", keys_pool_scales, offsets[:], SLOTS, U8)
+        keys_g = gather("keys_g", keys_pool, offsets[:], SLOTS, U32)
+        a = ps.tile([P, SLOTS], F32, name="a")
+        mx_product(a[:], q_codes[:], q_scales[:], keys_g[:], keys_scales_g[:])
+
+        stats = tile("stats", [P, 8], F32)
+        below = tile("below", [P, SLOTS], F32)
+        nc.scalar.activation(out=below[:], in_=a[:], func=ACT.Relu, bias=th_cap[:], scale=-1.0)
+        capped = tile("capped", [P, SLOTS], F32)
+        nc.scalar.activation(out=capped[:], in_=below[:], func=ACT.Exp, bias=CAP, scale=-1.0)
+        soft = tile("soft", [P, SLOTS], F32)
+        nc.scalar.activation(out=soft[:], in_=capped[:], func=ACT.Ln, bias=1.0)
+
+        p_sb = tile("p_sb", [P, SLOTS], F32)
+        for h in range(HALVES):
+            part = slice(h * HALF, (h + 1) * HALF)
+            nc.vector.scalar_tensor_tensor(out=p_sb[:, part].rearrange("p (j g) -> p j g", j=GROUP),
+                                           in0=a[:, part].rearrange("p (g j) -> p j g", j=GROUP), scalar=th_sb[:],
+                                           in1=soft[:, part].rearrange("p (g j) -> p j g", j=GROUP),
+                                           op0=ALU.subtract, op1=ALU.max, accum_out=stats[:, h : h + 1])
+        sig = tile("sig", [P, SLOTS], F32)
+        nc.scalar.activation(out=sig[:], in_=a[:], func=ACT.Sigmoid, bias=neg_th[:])
+        nc.vector.tensor_scalar(out=stats[:, 2:3], in0=stats[:, 0:1], scalar1=stats[:, 1:2], scalar2=reserve_sb[:],
+                                op0=ALU.add, op1=ALU.add)
+        nc.vector.reciprocal(out=stats[:, 4:5], in_=stats[:, 2:3])
+        nc.vector.tensor_scalar(out=stats[:, 3:4], in0=stats[:, 4:5], scalar1=512.0, scalar2=None, op0=ALU.mult)
+
+        factor = []
+        for h in range(HALVES):
+            inv_turned = tile(f"inv_turned{h}", [P, P], F32)
+            nc.vector.reciprocal(out=inv_turned[:], in_=sums[h][:, 0, :])
+            nc.tensor.transpose(sums[h][:, 1, :], inv_turned[:], ident[:])
+        g_codes, g_scales = quantize("g", interleave_rows("g_grouped", g_raw), Q)
+        c0 = ps.tile([P, SLOTS], F32, name="c0")
+        hs = []
+        for h in range(HALVES):
+            fac = tile(f"factor{h}", [P, P], F32)
+            nc.vector.tensor_tensor(out=fac[:], in0=sums[h][:, 1, :], in1=hsc4[:].rearrange("p b t i -> p (b t i)"), op=ALU.mult)
+            factor.append(fac)
+        for h in range(HALVES):
+            hs.append(tile(f"hs{h}", [P, GROUP, RUNS, RUN, PACK], BF16))
+            nc.vector.tensor_tensor(
+                out=hs[h][:].rearrange("p j b i t -> p j b t i"), in0=ht[h][:],
+                in1=factor[h][:].rearrange("p (b t i) -> p b t i", t=PACK, i=RUN).unsqueeze(1).to_broadcast([P, GROUP, RUNS, PACK, RUN]),
+                op=ALU.mult)
+        for h in range(HALVES):
+            hs_codes, hs_scales = quantize(f"hs{h}", hs[h][:].rearrange("p j b i t -> p (j b i t)"), HALF)
+            mx_product(c0[:, h * HALF : (h + 1) * HALF], g_codes[:], g_scales[:], hs_codes[:], hs_scales[:])
+
+        junk = tile("weighted", [P, SLOTS], F32)
+        nc.vector.scalar_tensor_tensor(out=junk[:], in0=c0[:], scalar=stats[:, 4:5], in1=p_sb[:], op0=ALU.mult,
+                                       op1=ALU.mult, accum_out=stats[:, 5:6])
+        dp = tile("dp", [P, HALVES, HALF // GROUP, GROUP], F32)
+        nc.vector.tensor_scalar(out=dp[:], in0=c0[:].rearrange("p (h j g) -> p h g j", h=HALVES, j=GROUP),
+                                scalar1=stats[:, 5:6], scalar2=stats[:, 3:4], op0=ALU.subtract, op1=ALU.mult)
+        nc.vector.tensor_tensor(out=scattered[:].indirect(offsets[:]), in0=dp[:].rearrange("p h g j -> p (h g j)"),
+                                in1=sig[:], op=ALU.mult)
+        width = T // OUT_CHUNKS
+        for c in range(OUT_CHUNKS):
+            part = slice(c * width, (c + 1) * width)
+            res = tile(f"res{c}", [P, width], F32)
+            nc.vector.tensor_tensor(out=res[:], in0=old_sb[:, part], in1=scattered[:, part], op=ALU.add)
+            nc.sync.dma_start(out=out[:, part], in_=res[:])

@@ -39,23 +39,24 @@ def tile_attend_blrshared_capped_kernel(tc, query, keys_words, keys_scales, th, 
         def tile(name, shape, dtype, tag=None):
             return sb.tile(shape, dtype, name=name, tag=tag or name, align_bytes=64)
 
-        def load_words(name, words, tag):
-            pool_words = tile(name, [P, T], U32, tag)
+        def load_words(name, words):
+            pool_words = tile(name, [P, T], U32)
             nc.sync.dma_start(out=pool_words[:].bitcast(I32), in_=words[0].rearrange("p n t -> p (n t)").bitcast(I32))
             return pool_words
 
-        def load_scales(pool_scales, scales, queue):
+        def load_scales(pool_scales, scales):
             for quad in range(4):
-                queue.dma_start(out=pool_scales[32 * quad : 32 * quad + 4, :].bitcast(I32),
-                                    in_=scales[0, 4 * quad : 4 * quad + 4, :].bitcast(I32))
+                rows = scales[0, 4 * quad : 4 * quad + 4, :].bitcast(I32)
+                nc.sync.dma_start(out=pool_scales[32 * quad : 32 * quad + 32, :].bitcast(I32),
+                                  in_=rows.unsqueeze(0).to_broadcast([8, 4, T // 4]))
 
         def load_column(name, vec, width, queue):
             col = tile(name, [P, width], F32)
             queue.dma_start(out=col[:], in_=vec.rearrange("(p t) o -> p (t o)", t=width))
             return col
 
-        def load_rows(name, mat, width, tag):
-            raw = tile(name, [P, PACK, width], F32, tag)
+        def load_rows(name, mat, width):
+            raw = tile(name, [P, PACK, width], F32)
             nc.sync.dma_start(out=raw[:], in_=mat.rearrange("(p j) c -> p j c", j=PACK))
             return raw
 
@@ -74,46 +75,47 @@ def tile_attend_blrshared_capped_kernel(tc, query, keys_words, keys_scales, th, 
             nc.tensor.matmul_mx(out=acc, lhsT=lhs_codes.bitcast(FP8X4), lhsT_scale=lhs_scales,
                                 rhs=rhs_codes.bitcast(FP8X4), rhs_scale=rhs_scales, start=True, stop=True)
 
-        def interleave_rows(name, raw):
+        def interleave_rows(name, raw, copy):
             grouped = tile(name, [P, Q, PACK], BF16)
-            nc.vector.tensor_copy(out=grouped[:].rearrange("p (c i) j -> p c j i", i=4),
-                                  in_=raw[:].rearrange("p j (c i) -> p c j i", i=4))
+            copy(out=grouped[:].rearrange("p (c i) j -> p c j i", i=4),
+                 in_=raw[:].rearrange("p j (c i) -> p c j i", i=4))
             return grouped[:].rearrange("p q j -> p (q j)")
 
         offsets = sb.tile([P, SLOTS // 16], U16, name="offsets")
         nc.sync.dma_start(offsets[:], offs)
         tab_pool_scales = tile("tab_pool_scales", [P, T], U8)
         keys_pool_scales = tile("keys_pool_scales", [P, T], U8)
-        nc.vector.memset(tab_pool_scales[:].bitcast(I32), 0)
-        nc.vector.memset(keys_pool_scales[:].bitcast(I32), 0)
-        load_scales(tab_pool_scales, tab_scales, nc.scalar)
-        w_raw = load_rows("w_raw", w1, R, "big0")
-        tab_pool = load_words("tab_pool", tab_words, "big1")
-        temper_sb = load_column("temper_sb", temper, PACK, nc.gpsimd)
-        th_sb = load_column("th_sb", th, 1, nc.gpsimd)
-        hsc_sb = load_column("hsc_sb", hsc, PACK, nc.gpsimd)
-        reserve_sb = load_column("reserve_sb", reserve, 1, nc.gpsimd)
-        q_raw = load_rows("q_raw", query, Q, "rows")
-        load_scales(keys_pool_scales, keys_scales, nc.sync)
+        load_scales(tab_pool_scales, tab_scales)
+        w_raw = load_rows("w_raw", w1, R)
+        temper_sb = load_column("temper_sb", temper, PACK, nc.sync)
+        tab_pool = load_words("tab_pool", tab_words)
+        q_raw = load_rows("q_raw", query, Q)
+        load_scales(keys_pool_scales, keys_scales)
+        keys_pool = load_words("keys_pool", keys_words)
+        th_sb = load_column("th_sb", th, 1, nc.sync)
+        hsc_sb = load_column("hsc_sb", hsc, PACK, nc.sync)
+        reserve_sb = load_column("reserve_sb", reserve, 1, nc.sync)
+        g_raw = load_rows("g_raw", gout, Q)
+        old_sb = tile("old_sb", [P, T], F32)
+        nc.sync.dma_start(out=old_sb[:], in_=old)
 
         ident = tile("ident", [P, P], F32)
         make_identity(nc, ident[:])
         scattered = tile("scattered", [P, T], F32)
         nc.vector.memset(scattered[:], 0.0)
 
-        neg_th = tile("neg_th", [P, 1], F32)
-        nc.scalar.activation(out=neg_th[:], in_=th_sb[:], func=ACT.Identity, scale=-1.0)
         th_cap = tile("th_cap", [P, 1], F32)
-        nc.scalar.activation(out=th_cap[:], in_=th_sb[:], func=ACT.Identity, bias=CAP)
+        nc.gpsimd.tensor_scalar(out=th_cap[:], in0=th_sb[:], scalar1=CAP, scalar2=1.0, op0=ALU.add, op1=ALU.mult)
+        neg_th = tile("neg_th", [P, 1], F32)
+        nc.gpsimd.tensor_scalar(out=neg_th[:], in0=th_sb[:], scalar1=-1.0, scalar2=0.0, op0=ALU.mult, op1=ALU.add)
         hsc4 = tile("hsc4", [P, RUNS, PACK, RUN], F32)
-        nc.scalar.activation(out=hsc4[:], in_=hsc_sb[:].unsqueeze(1).unsqueeze(3).to_broadcast([P, RUNS, PACK, RUN]),
-                             func=ACT.Identity, scale=4.0)
+        nc.gpsimd.tensor_scalar(out=hsc4[:], in0=hsc_sb[:].unsqueeze(1).unsqueeze(3).to_broadcast([P, RUNS, PACK, RUN]),
+                                scalar1=4.0, scalar2=0.0, op0=ALU.mult, op1=ALU.add)
 
         tab_scales_g = gather("tab_scales_g", tab_pool_scales, offsets[:], SLOTS, U8)
         w_grouped = tile("w_grouped", [P, PACK, P, PACK], BF16)
         nc.vector.tensor_copy(out=w_grouped[:].rearrange("p t m j -> p m j t"),
                               in_=w_raw[:].rearrange("p j (m t) -> p m j t", t=PACK))
-        keys_pool = load_words("keys_pool", keys_words, "big0")
         w_codes, w_scales = quantize("w", w_grouped[:].rearrange("p t m j -> p (t m j)"), R)
 
         cols = HALF // 16
@@ -141,67 +143,81 @@ def tile_attend_blrshared_capped_kernel(tc, query, keys_words, keys_scales, th, 
                                  is_transpose=True, start=(j == 0), stop=(j == GROUP - 1))
             sums.append(turn)
 
-        q_codes, q_scales = quantize("q", interleave_rows("q_grouped", q_raw), Q)
-        g_raw = load_rows("g_raw", gout, Q, "rows")
-        old_sb = tile("old_sb", [P, T], F32, "big1")
-        nc.sync.dma_start(out=old_sb[:], in_=old)
+        q_codes, q_scales = quantize("q", interleave_rows("q_grouped", q_raw, nc.vector.tensor_copy), Q)
         keys_scales_g = gather("keys_scales_g", keys_pool_scales, offsets[:], SLOTS, U8)
-        keys_g = gather("keys_g", keys_pool, offsets[:], SLOTS, U32)
-        a = ps.tile([P, SLOTS], F32, name="a")
-        mx_product(a[:], q_codes[:], q_scales[:], keys_g[:], keys_scales_g[:])
-
+        g_grouped = interleave_rows("g_grouped", g_raw, nc.scalar.copy)
         stats = tile("stats", [P, 8], F32)
-        below = tile("below", [P, SLOTS], F32)
-        nc.scalar.activation(out=below[:], in_=a[:], func=ACT.Relu, bias=th_cap[:], scale=-1.0)
+        below = tile("below", [P, HALVES, GROUP, HALF // GROUP], F32)
         capped = tile("capped", [P, SLOTS], F32)
-        nc.scalar.activation(out=capped[:], in_=below[:], func=ACT.Exp, bias=CAP, scale=-1.0)
+        a = []
+        for h in range(HALVES):
+            part = slice(h * HALF, (h + 1) * HALF)
+            keys_g = gather(f"keys_g{h}", keys_pool, offsets[:, h * cols : (h + 1) * cols], HALF, U32)
+            a.append(ps.tile([P, HALF], F32, name=f"a{h}"))
+            mx_product(a[h][:], q_codes[:], q_scales[:], keys_g[:], keys_scales_g[:, part])
+            nc.scalar.activation(out=below[:, h], in_=a[h][:].rearrange("p (g j) -> p j g", j=GROUP), func=ACT.Relu,
+                                 bias=th_cap[:], scale=-1.0)
+            nc.scalar.activation(out=capped[:, part], in_=below[:, h].rearrange("p j g -> p (j g)"), func=ACT.Exp,
+                                 bias=CAP, scale=-1.0)
         soft = tile("soft", [P, SLOTS], F32)
         nc.scalar.activation(out=soft[:], in_=capped[:], func=ACT.Ln, bias=1.0)
 
-        p_sb = tile("p_sb", [P, SLOTS], F32)
-        for h in range(HALVES):
-            part = slice(h * HALF, (h + 1) * HALF)
-            nc.vector.scalar_tensor_tensor(out=p_sb[:, part].rearrange("p (j g) -> p j g", j=GROUP),
-                                           in0=a[:, part].rearrange("p (g j) -> p j g", j=GROUP), scalar=th_sb[:],
-                                           in1=soft[:, part].rearrange("p (g j) -> p j g", j=GROUP),
-                                           op0=ALU.subtract, op1=ALU.max, accum_out=stats[:, h : h + 1])
-        sig = tile("sig", [P, SLOTS], F32)
-        nc.scalar.activation(out=sig[:], in_=a[:], func=ACT.Sigmoid, bias=neg_th[:])
-        nc.vector.tensor_scalar(out=stats[:, 2:3], in0=stats[:, 0:1], scalar1=stats[:, 1:2], scalar2=reserve_sb[:],
-                                op0=ALU.add, op1=ALU.add)
-        nc.vector.reciprocal(out=stats[:, 4:5], in_=stats[:, 2:3])
-        nc.vector.tensor_scalar(out=stats[:, 3:4], in0=stats[:, 4:5], scalar1=512.0, scalar2=None, op0=ALU.mult)
-
         factor = []
+        inv_turned = tile("inv_turned", [P, HALVES, P], F32, "keys_pool")
         for h in range(HALVES):
-            inv_turned = tile(f"inv_turned{h}", [P, P], F32)
-            nc.vector.reciprocal(out=inv_turned[:], in_=sums[h][:, 0, :])
-            nc.tensor.transpose(sums[h][:, 1, :], inv_turned[:], ident[:])
-        g_codes, g_scales = quantize("g", interleave_rows("g_grouped", g_raw), Q)
-        c0 = ps.tile([P, SLOTS], F32, name="c0")
+            nc.vector.reciprocal(out=inv_turned[:, h, :], in_=sums[h][:, 0, :])
+            nc.tensor.transpose(sums[h][:, 1, :], inv_turned[:, h, :], ident[:])
+        g_codes, g_scales = quantize("g", g_grouped, Q)
         hs = []
         for h in range(HALVES):
             fac = tile(f"factor{h}", [P, P], F32)
             nc.vector.tensor_tensor(out=fac[:], in0=sums[h][:, 1, :], in1=hsc4[:].rearrange("p b t i -> p (b t i)"), op=ALU.mult)
             factor.append(fac)
-        for h in range(HALVES):
-            hs.append(tile(f"hs{h}", [P, GROUP, RUNS, RUN, PACK], BF16))
+        def normalise(h):
+            hs.append(tile(f"hs{h}", [P, GROUP, RUNS, RUN, PACK], BF16, "soft" if h == 1 else None))
             nc.vector.tensor_tensor(
                 out=hs[h][:].rearrange("p j b i t -> p j b t i"), in0=ht[h][:],
                 in1=factor[h][:].rearrange("p (b t i) -> p b t i", t=PACK, i=RUN).unsqueeze(1).to_broadcast([P, GROUP, RUNS, PACK, RUN]),
                 op=ALU.mult)
+
+        normalise(0)
+        p_sb = tile("p_sb", [P, SLOTS], F32, "ht0")
+        for h in range(HALVES):
+            part = slice(h * HALF, (h + 1) * HALF)
+            nc.vector.scalar_tensor_tensor(out=p_sb[:, part].rearrange("p (j g) -> p j g", j=GROUP),
+                                           in0=a[h][:].rearrange("p (g j) -> p j g", j=GROUP), scalar=th_sb[:],
+                                           in1=soft[:, part].rearrange("p (j g) -> p j g", j=GROUP),
+                                           op0=ALU.subtract, op1=ALU.max, accum_out=stats[:, h : h + 1])
+        sig = tile("sig", [P, SLOTS], F32)
+        for h in range(HALVES):
+            nc.scalar.activation(out=sig[:, h * HALF : (h + 1) * HALF], in_=a[h][:], func=ACT.Sigmoid, bias=neg_th[:])
+        nc.vector.tensor_scalar(out=stats[:, 2:3], in0=stats[:, 0:1], scalar1=stats[:, 1:2], scalar2=reserve_sb[:],
+                                op0=ALU.add, op1=ALU.add)
+        nc.vector.reciprocal(out=stats[:, 4:5], in_=stats[:, 2:3])
+        nc.vector.tensor_scalar(out=stats[:, 3:4], in0=stats[:, 4:5], scalar1=512.0, scalar2=None, op0=ALU.mult)
+        nc.vector.tensor_scalar(out=stats[:, 5:6], in0=stats[:, 4:5], scalar1=stats[:, 4:5], scalar2=512.0,
+                                op0=ALU.mult, op1=ALU.mult)
+        normalise(1)
+        c0 = []
         for h in range(HALVES):
             hs_codes, hs_scales = quantize(f"hs{h}", hs[h][:].rearrange("p j b i t -> p (j b i t)"), HALF)
-            mx_product(c0[:, h * HALF : (h + 1) * HALF], g_codes[:], g_scales[:], hs_codes[:], hs_scales[:])
-
-        junk = tile("weighted", [P, SLOTS], F32)
-        nc.vector.scalar_tensor_tensor(out=junk[:], in0=c0[:], scalar=stats[:, 4:5], in1=p_sb[:], op0=ALU.mult,
-                                       op1=ALU.mult, accum_out=stats[:, 5:6])
-        dp = tile("dp", [P, HALVES, HALF // GROUP, GROUP], F32)
-        nc.vector.tensor_scalar(out=dp[:], in0=c0[:].rearrange("p (h j g) -> p h g j", h=HALVES, j=GROUP),
-                                scalar1=stats[:, 5:6], scalar2=stats[:, 3:4], op0=ALU.subtract, op1=ALU.mult)
-        nc.vector.tensor_tensor(out=scattered[:].indirect(offsets[:]), in0=dp[:].rearrange("p h g j -> p (h g j)"),
-                                in1=sig[:], op=ALU.mult)
+            c0.append(ps.tile([P, HALF], F32, name=f"c0{h}", tag=f"zh0{h}"))
+            mx_product(c0[h][:], g_codes[:], g_scales[:], hs_codes[:], hs_scales[:])
+        weighted = tile("weighted", [P, SLOTS], F32)
+        scaled = tile("scaled", [P, HALVES, HALF // GROUP, GROUP], F32)
+        for h in range(HALVES):
+            part = slice(h * HALF, (h + 1) * HALF)
+            nc.vector.scalar_tensor_tensor(out=weighted[:, part], in0=c0[h][:], scalar=stats[:, 5:6], in1=p_sb[:, part],
+                                           op0=ALU.mult, op1=ALU.mult, accum_out=stats[:, 6 + h : 7 + h])
+            nc.scalar.activation(out=scaled[:, h], in_=c0[h][:].rearrange("p (j g) -> p g j", j=GROUP), func=ACT.Identity,
+                                 scale=stats[:, 3:4])
+        dp = tile("dp", [P, SLOTS], F32)
+        for h in range(HALVES):
+            part = slice(h * HALF, (h + 1) * HALF)
+            nc.vector.tensor_scalar(out=dp[:, part], in0=scaled[:, h].rearrange("p g j -> p (g j)"), scalar1=stats[:, 6:7],
+                                    scalar2=stats[:, 7:8], op0=ALU.subtract, op1=ALU.subtract)
+            nc.vector.tensor_tensor(out=scattered[:].indirect(offsets[:, h * cols : (h + 1) * cols]), in0=dp[:, part],
+                                    in1=sig[:, part], op=ALU.mult)
         width = T // OUT_CHUNKS
         for c in range(OUT_CHUNKS):
             part = slice(c * width, (c + 1) * width)

@@ -26,6 +26,8 @@ RUN = 4
 RUNS = HALF // GROUP // RUN
 OUT_CHUNKS = 4
 CAP = 32.0
+W_SPLIT = 88
+OUT_EDGES = (0, 256, 768, 1280, 1792, 2048)
 FLOPS = 2 * 512 * SLOTS * (Q + R + Q)
 
 
@@ -83,17 +85,17 @@ def tile_attend_blrshared_capped_kernel(tc, query, keys_words, keys_scales, th, 
 
         offsets = sb.tile([P, SLOTS // 16], U16, name="offsets")
         nc.sync.dma_start(offsets[:], offs)
+        th_sb = load_column("th_sb", th, 1, nc.sync)
+        hsc_sb = load_column("hsc_sb", hsc, PACK, nc.sync)
         tab_pool_scales = tile("tab_pool_scales", [P, T], U8)
         keys_pool_scales = tile("keys_pool_scales", [P, T], U8)
         load_scales(tab_pool_scales, tab_scales)
         w_raw = load_rows("w_raw", w1, R)
-        temper_sb = load_column("temper_sb", temper, PACK, nc.sync)
         tab_pool = load_words("tab_pool", tab_words)
+        temper_sb = load_column("temper_sb", temper, PACK, nc.sync)
         q_raw = load_rows("q_raw", query, Q)
         load_scales(keys_pool_scales, keys_scales)
         keys_pool = load_words("keys_pool", keys_words)
-        th_sb = load_column("th_sb", th, 1, nc.sync)
-        hsc_sb = load_column("hsc_sb", hsc, PACK, nc.sync)
         reserve_sb = load_column("reserve_sb", reserve, 1, nc.sync)
         g_raw = load_rows("g_raw", gout, Q)
         old_sb = tile("old_sb", [P, T], F32)
@@ -105,17 +107,18 @@ def tile_attend_blrshared_capped_kernel(tc, query, keys_words, keys_scales, th, 
         nc.vector.memset(scattered[:], 0.0)
 
         th_cap = tile("th_cap", [P, 1], F32)
-        nc.gpsimd.tensor_scalar(out=th_cap[:], in0=th_sb[:], scalar1=CAP, scalar2=1.0, op0=ALU.add, op1=ALU.mult)
+        nc.scalar.activation(out=th_cap[:], in_=th_sb[:], func=ACT.Identity, bias=CAP)
         neg_th = tile("neg_th", [P, 1], F32)
-        nc.gpsimd.tensor_scalar(out=neg_th[:], in0=th_sb[:], scalar1=-1.0, scalar2=0.0, op0=ALU.mult, op1=ALU.add)
+        nc.scalar.activation(out=neg_th[:], in_=th_sb[:], func=ACT.Identity, scale=-1.0)
         hsc4 = tile("hsc4", [P, RUNS, PACK, RUN], F32)
-        nc.gpsimd.tensor_scalar(out=hsc4[:], in0=hsc_sb[:].unsqueeze(1).unsqueeze(3).to_broadcast([P, RUNS, PACK, RUN]),
-                                scalar1=4.0, scalar2=0.0, op0=ALU.mult, op1=ALU.add)
+        nc.scalar.activation(out=hsc4[:], in_=hsc_sb[:].unsqueeze(1).unsqueeze(3).to_broadcast([P, RUNS, PACK, RUN]),
+                             func=ACT.Identity, scale=4.0)
 
         tab_scales_g = gather("tab_scales_g", tab_pool_scales, offsets[:], SLOTS, U8)
         w_grouped = tile("w_grouped", [P, PACK, P, PACK], BF16)
-        nc.vector.tensor_copy(out=w_grouped[:].rearrange("p t m j -> p m j t"),
-                              in_=w_raw[:].rearrange("p j (m t) -> p m j t", t=PACK))
+        for copy, part in ((nc.vector.tensor_copy, slice(0, W_SPLIT)), (nc.scalar.copy, slice(W_SPLIT, P))):
+            copy(out=w_grouped[:].rearrange("p t m j -> p m j t")[:, part],
+                 in_=w_raw[:].rearrange("p j (m t) -> p m j t", t=PACK)[:, part])
         w_codes, w_scales = quantize("w", w_grouped[:].rearrange("p t m j -> p (t m j)"), R)
 
         cols = HALF // 16
@@ -197,12 +200,16 @@ def tile_attend_blrshared_capped_kernel(tc, query, keys_words, keys_scales, th, 
         nc.vector.tensor_scalar(out=stats[:, 3:4], in0=stats[:, 4:5], scalar1=512.0, scalar2=None, op0=ALU.mult)
         nc.vector.tensor_scalar(out=stats[:, 5:6], in0=stats[:, 4:5], scalar1=stats[:, 4:5], scalar2=512.0,
                                 op0=ALU.mult, op1=ALU.mult)
-        normalise(1)
         c0 = []
-        for h in range(HALVES):
+
+        def read_gradient(h):
             hs_codes, hs_scales = quantize(f"hs{h}", hs[h][:].rearrange("p j b i t -> p (j b i t)"), HALF)
             c0.append(ps.tile([P, HALF], F32, name=f"c0{h}", tag=f"zh0{h}"))
             mx_product(c0[h][:], g_codes[:], g_scales[:], hs_codes[:], hs_scales[:])
+
+        read_gradient(0)
+        normalise(1)
+        read_gradient(1)
         weighted = tile("weighted", [P, SLOTS], F32)
         scaled = tile("scaled", [P, HALVES, HALF // GROUP, GROUP], F32)
         for h in range(HALVES):
@@ -218,9 +225,8 @@ def tile_attend_blrshared_capped_kernel(tc, query, keys_words, keys_scales, th, 
                                     scalar2=stats[:, 7:8], op0=ALU.subtract, op1=ALU.subtract)
             nc.vector.tensor_tensor(out=scattered[:].indirect(offsets[:, h * cols : (h + 1) * cols]), in0=dp[:, part],
                                     in1=sig[:, part], op=ALU.mult)
-        width = T // OUT_CHUNKS
-        for c in range(OUT_CHUNKS):
-            part = slice(c * width, (c + 1) * width)
-            res = tile(f"res{c}", [P, width], F32)
+        for c, (lo, hi) in enumerate(zip(OUT_EDGES, OUT_EDGES[1:])):
+            part = slice(lo, hi)
+            res = tile(f"res{c}", [P, hi - lo], F32)
             nc.vector.tensor_tensor(out=res[:], in0=old_sb[:, part], in1=scattered[:, part], op=ALU.add)
             nc.sync.dma_start(out=out[:, part], in_=res[:])

@@ -26,7 +26,6 @@ RUN = 4
 RUNS = HALF // GROUP // RUN
 OUT_CHUNKS = 4
 CAP = 32.0
-W_SPLIT = 88
 OUT_EDGES = (0, 256, 768, 1280, 1792, 2048)
 FLOPS = 2 * 512 * SLOTS * (Q + R + Q)
 
@@ -41,24 +40,26 @@ def tile_attend_blrshared_capped_kernel(tc, query, keys_words, keys_scales, th, 
         def tile(name, shape, dtype, tag=None):
             return sb.tile(shape, dtype, name=name, tag=tag or name, align_bytes=64)
 
-        def load_words(name, words):
-            pool_words = tile(name, [P, T], U32)
+        def load_words(name, words, tag=None):
+            pool_words = tile(name, [P, T], U32, tag)
             nc.sync.dma_start(out=pool_words[:].bitcast(I32), in_=words[0].rearrange("p n t -> p (n t)").bitcast(I32))
             return pool_words
 
-        def load_scales(pool_scales, scales):
+        def load_scales(name, scales):
+            pool_scales = tile(name, [P, T], U8)
+            nc.vector.memset(pool_scales[:].bitcast(I32), 0)
             for quad in range(4):
-                rows = scales[0, 4 * quad : 4 * quad + 4, :].bitcast(I32)
-                nc.sync.dma_start(out=pool_scales[32 * quad : 32 * quad + 32, :].bitcast(I32),
-                                  in_=rows.unsqueeze(0).to_broadcast([8, 4, T // 4]))
+                nc.scalar.dma_start(out=pool_scales[32 * quad : 32 * quad + 4, :].bitcast(I32),
+                                    in_=scales[0, 4 * quad : 4 * quad + 4, :].bitcast(I32))
+            return pool_scales
 
-        def load_column(name, vec, width, queue):
-            col = tile(name, [P, width], F32)
-            queue.dma_start(out=col[:], in_=vec.rearrange("(p t) o -> p (t o)", t=width))
+        def load_column(name, vec, width, tag=None):
+            col = tile(name, [P, width], F32, tag)
+            nc.sync.dma_start(out=col[:], in_=vec.rearrange("(p t) o -> p (t o)", t=width))
             return col
 
-        def load_rows(name, mat, width):
-            raw = tile(name, [P, PACK, width], F32)
+        def load_rows(name, mat, width, tag=None):
+            raw = tile(name, [P, PACK, width], F32, tag)
             nc.sync.dma_start(out=raw[:], in_=mat.rearrange("(p j) c -> p j c", j=PACK))
             return raw
 
@@ -68,8 +69,8 @@ def tile_attend_blrshared_capped_kernel(tc, query, keys_words, keys_scales, th, 
             nc.vector.quantize_mx(out=codes[:].bitcast(FP8X4), scales=scales[:], in_=grouped)
             return codes, scales
 
-        def gather(name, window, offsets, width, dtype):
-            picked = tile(name, [P, width], dtype)
+        def gather(name, window, offsets, width, dtype, tag=None):
+            picked = tile(name, [P, width], dtype, tag)
             nc.vector.tensor_copy(out=picked[:], in_=window[:].indirect(offsets))
             return picked
 
@@ -77,49 +78,46 @@ def tile_attend_blrshared_capped_kernel(tc, query, keys_words, keys_scales, th, 
             nc.tensor.matmul_mx(out=acc, lhsT=lhs_codes.bitcast(FP8X4), lhsT_scale=lhs_scales,
                                 rhs=rhs_codes.bitcast(FP8X4), rhs_scale=rhs_scales, start=True, stop=True)
 
-        def interleave_rows(name, raw, copy):
-            grouped = tile(name, [P, Q, PACK], BF16)
+        def interleave_rows(name, raw, copy, tag=None):
+            grouped = tile(name, [P, Q, PACK], BF16, tag)
             copy(out=grouped[:].rearrange("p (c i) j -> p c j i", i=4),
                  in_=raw[:].rearrange("p j (c i) -> p c j i", i=4))
             return grouped[:].rearrange("p q j -> p (q j)")
 
         offsets = sb.tile([P, SLOTS // 16], U16, name="offsets")
         nc.sync.dma_start(offsets[:], offs)
-        th_sb = load_column("th_sb", th, 1, nc.sync)
-        hsc_sb = load_column("hsc_sb", hsc, PACK, nc.sync)
-        tab_pool_scales = tile("tab_pool_scales", [P, T], U8)
-        keys_pool_scales = tile("keys_pool_scales", [P, T], U8)
-        load_scales(tab_pool_scales, tab_scales)
+        th_sb = load_column("th_sb", th, 1)
+        hsc_sb = load_column("hsc_sb", hsc, PACK)
+        temper_sb = load_column("temper_sb", temper, PACK)
         w_raw = load_rows("w_raw", w1, R)
         tab_pool = load_words("tab_pool", tab_words)
-        temper_sb = load_column("temper_sb", temper, PACK, nc.sync)
-        q_raw = load_rows("q_raw", query, Q)
-        load_scales(keys_pool_scales, keys_scales)
-        keys_pool = load_words("keys_pool", keys_words)
-        reserve_sb = load_column("reserve_sb", reserve, 1, nc.sync)
-        g_raw = load_rows("g_raw", gout, Q)
-        old_sb = tile("old_sb", [P, T], F32)
-        nc.sync.dma_start(out=old_sb[:], in_=old)
+        tab_pool_scales = load_scales("tab_pool_scales", tab_scales)
+
+        hsc4 = tile("hsc4", [P, RUNS, PACK, RUN], F32)
+        nc.scalar.activation(out=hsc4[:], in_=hsc_sb[:].unsqueeze(1).unsqueeze(3).to_broadcast([P, RUNS, PACK, RUN]),
+                             func=ACT.Identity, scale=4.0)
+        th_cap = tile("th_cap", [P, 1], F32)
+        nc.scalar.activation(out=th_cap[:], in_=th_sb[:], func=ACT.Identity, bias=CAP)
+        neg_th = tile("neg_th", [P, 1], F32)
+        nc.scalar.activation(out=neg_th[:], in_=th_sb[:], func=ACT.Identity, scale=-1.0)
+        q_raw = load_rows("q_raw", query, Q, "hsc_sb")
+        keys_pool = load_words("keys_pool", keys_words, "th_sb")
 
         ident = tile("ident", [P, P], F32)
         make_identity(nc, ident[:])
         scattered = tile("scattered", [P, T], F32)
         nc.vector.memset(scattered[:], 0.0)
-
-        th_cap = tile("th_cap", [P, 1], F32)
-        nc.scalar.activation(out=th_cap[:], in_=th_sb[:], func=ACT.Identity, bias=CAP)
-        neg_th = tile("neg_th", [P, 1], F32)
-        nc.scalar.activation(out=neg_th[:], in_=th_sb[:], func=ACT.Identity, scale=-1.0)
-        hsc4 = tile("hsc4", [P, RUNS, PACK, RUN], F32)
-        nc.scalar.activation(out=hsc4[:], in_=hsc_sb[:].unsqueeze(1).unsqueeze(3).to_broadcast([P, RUNS, PACK, RUN]),
-                             func=ACT.Identity, scale=4.0)
+        keys_pool_scales = load_scales("keys_pool_scales", keys_scales)
 
         tab_scales_g = gather("tab_scales_g", tab_pool_scales, offsets[:], SLOTS, U8)
+        g_raw = load_rows("g_raw", gout, Q, "tab_pool_scales")
         w_grouped = tile("w_grouped", [P, PACK, P, PACK], BF16)
-        for copy, part in ((nc.vector.tensor_copy, slice(0, W_SPLIT)), (nc.scalar.copy, slice(W_SPLIT, P))):
-            copy(out=w_grouped[:].rearrange("p t m j -> p m j t")[:, part],
-                 in_=w_raw[:].rearrange("p j (m t) -> p m j t", t=PACK)[:, part])
+        nc.vector.tensor_copy(out=w_grouped[:].rearrange("p t m j -> p m j t"),
+                              in_=w_raw[:].rearrange("p j (m t) -> p m j t", t=PACK))
+        old_sb = tile("old_sb", [P, T], F32, "w_raw")
+        nc.sync.dma_start(out=old_sb[:], in_=old)
         w_codes, w_scales = quantize("w", w_grouped[:].rearrange("p t m j -> p (t m j)"), R)
+        reserve_sb = load_column("reserve_sb", reserve, 1, "w_grouped")
 
         cols = HALF // 16
         ht = []
@@ -147,8 +145,7 @@ def tile_attend_blrshared_capped_kernel(tc, query, keys_words, keys_scales, th, 
             sums.append(turn)
 
         q_codes, q_scales = quantize("q", interleave_rows("q_grouped", q_raw, nc.vector.tensor_copy), Q)
-        keys_scales_g = gather("keys_scales_g", keys_pool_scales, offsets[:], SLOTS, U8)
-        g_grouped = interleave_rows("g_grouped", g_raw, nc.scalar.copy)
+        keys_scales_g = gather("keys_scales_g", keys_pool_scales, offsets[:], SLOTS, U8, "tab_pool")
         stats = tile("stats", [P, 8], F32)
         below = tile("below", [P, HALVES, GROUP, HALF // GROUP], F32)
         capped = tile("capped", [P, SLOTS], F32)
@@ -164,13 +161,13 @@ def tile_attend_blrshared_capped_kernel(tc, query, keys_words, keys_scales, th, 
                                  bias=CAP, scale=-1.0)
         soft = tile("soft", [P, SLOTS], F32)
         nc.scalar.activation(out=soft[:], in_=capped[:], func=ACT.Ln, bias=1.0)
+        g_grouped = interleave_rows("g_grouped", g_raw, nc.scalar.copy, "capped")
 
         factor = []
-        inv_turned = tile("inv_turned", [P, HALVES, P], F32, "keys_pool")
+        inv_turned = tile("inv_turned", [P, HALVES, P], F32, "th_sb")
         for h in range(HALVES):
             nc.vector.reciprocal(out=inv_turned[:, h, :], in_=sums[h][:, 0, :])
             nc.tensor.transpose(sums[h][:, 1, :], inv_turned[:, h, :], ident[:])
-        g_codes, g_scales = quantize("g", g_grouped, Q)
         hs = []
         for h in range(HALVES):
             fac = tile(f"factor{h}", [P, P], F32)
@@ -188,9 +185,9 @@ def tile_attend_blrshared_capped_kernel(tc, query, keys_words, keys_scales, th, 
         for h in range(HALVES):
             part = slice(h * HALF, (h + 1) * HALF)
             nc.vector.scalar_tensor_tensor(out=p_sb[:, part].rearrange("p (j g) -> p j g", j=GROUP),
-                                           in0=a[h][:].rearrange("p (g j) -> p j g", j=GROUP), scalar=th_sb[:],
+                                           in0=a[h][:].rearrange("p (g j) -> p j g", j=GROUP), scalar=neg_th[:],
                                            in1=soft[:, part].rearrange("p (j g) -> p j g", j=GROUP),
-                                           op0=ALU.subtract, op1=ALU.max, accum_out=stats[:, h : h + 1])
+                                           op0=ALU.add, op1=ALU.max, accum_out=stats[:, h : h + 1])
         sig = tile("sig", [P, SLOTS], F32)
         for h in range(HALVES):
             nc.scalar.activation(out=sig[:, h * HALF : (h + 1) * HALF], in_=a[h][:], func=ACT.Sigmoid, bias=neg_th[:])
@@ -200,6 +197,7 @@ def tile_attend_blrshared_capped_kernel(tc, query, keys_words, keys_scales, th, 
         nc.vector.tensor_scalar(out=stats[:, 3:4], in0=stats[:, 4:5], scalar1=512.0, scalar2=None, op0=ALU.mult)
         nc.vector.tensor_scalar(out=stats[:, 5:6], in0=stats[:, 4:5], scalar1=stats[:, 4:5], scalar2=512.0,
                                 op0=ALU.mult, op1=ALU.mult)
+        g_codes, g_scales = quantize("g", g_grouped, Q)
         c0 = []
 
         def read_gradient(h):

from contextlib import ExitStack

import concourse.mybir as mybir
from concourse.masks import make_identity

F32 = mybir.dt.float32
BF16 = mybir.dt.bfloat16
I32 = mybir.dt.int32
U32 = mybir.dt.uint32
U16 = mybir.dt.uint16
U8 = mybir.dt.uint8
FP8X4 = mybir.dt.float8_e4m3fn_x4
ALU = mybir.AluOpType
ACT = mybir.ActivationFunctionType

P = 128
PACK = 4
T = 2048
SLOTS = 512
Q = 128
R = 512
GROUP = 8
HALVES = 2
HALF = SLOTS // HALVES
RUN = 4
RUNS = HALF // GROUP // RUN
OUT_CHUNKS = 4
CAP = 32.0
OUT_EDGES = (0, 256, 768, 1280, 1792, 2048)
FLOPS = 2 * 512 * SLOTS * (Q + R + Q)


def tile_attend_blrshared_capped_kernel(tc, query, keys_words, keys_scales, th, reserve, tab_words, tab_scales,
                                         w1, temper, gout, hsc, old, offs, out):
    nc = tc.nc
    with ExitStack() as ctx:
        sb = ctx.enter_context(tc.tile_pool(name="sb", bufs=1))
        ps = ctx.enter_context(tc.psum_pool(name="ps", bufs=1))

        def tile(name, shape, dtype, tag=None):
            return sb.tile(shape, dtype, name=name, tag=tag or name, align_bytes=64)

        def load_words(name, words, tag=None):
            pool_words = tile(name, [P, T], U32, tag)
            nc.sync.dma_start(out=pool_words[:].bitcast(I32), in_=words[0].rearrange("p n t -> p (n t)").bitcast(I32))
            return pool_words

        def load_scales(name, scales):
            pool_scales = tile(name, [P, T], U8)
            nc.vector.memset(pool_scales[:].bitcast(I32), 0)
            for quad in range(4):
                nc.scalar.dma_start(out=pool_scales[32 * quad : 32 * quad + 4, :].bitcast(I32),
                                    in_=scales[0, 4 * quad : 4 * quad + 4, :].bitcast(I32))
            return pool_scales

        def load_column(name, vec, width, tag=None):
            col = tile(name, [P, width], F32, tag)
            nc.sync.dma_start(out=col[:], in_=vec.rearrange("(p t) o -> p (t o)", t=width))
            return col

        def load_rows(name, mat, width, tag=None):
            raw = tile(name, [P, PACK, width], F32, tag)
            nc.sync.dma_start(out=raw[:], in_=mat.rearrange("(p j) c -> p j c", j=PACK))
            return raw

        def quantize(name, grouped, width):
            codes = tile(name + "_codes", [P, width], U32)
            scales = tile(name + "_scales", [P, width], U8)
            nc.vector.quantize_mx(out=codes[:].bitcast(FP8X4), scales=scales[:], in_=grouped)
            return codes, scales

        def gather(name, window, offsets, width, dtype, tag=None):
            picked = tile(name, [P, width], dtype, tag)
            nc.vector.tensor_copy(out=picked[:], in_=window[:].indirect(offsets))
            return picked

        def mx_product(acc, lhs_codes, lhs_scales, rhs_codes, rhs_scales):
            nc.tensor.matmul_mx(out=acc, lhsT=lhs_codes.bitcast(FP8X4), lhsT_scale=lhs_scales,
                                rhs=rhs_codes.bitcast(FP8X4), rhs_scale=rhs_scales, start=True, stop=True)

        def interleave_rows(name, raw, copy, tag=None):
            grouped = tile(name, [P, Q, PACK], BF16, tag)
            copy(out=grouped[:].rearrange("p (c i) j -> p c j i", i=4),
                 in_=raw[:].rearrange("p j (c i) -> p c j i", i=4))
            return grouped[:].rearrange("p q j -> p (q j)")

        offsets = sb.tile([P, SLOTS // 16], U16, name="offsets")
        nc.sync.dma_start(offsets[:], offs)
        th_sb = load_column("th_sb", th, 1)
        hsc_sb = load_column("hsc_sb", hsc, PACK)
        temper_sb = load_column("temper_sb", temper, PACK)
        w_raw = load_rows("w_raw", w1, R)
        tab_pool = load_words("tab_pool", tab_words)
        tab_pool_scales = load_scales("tab_pool_scales", tab_scales)

        hsc4 = tile("hsc4", [P, RUNS, PACK, RUN], F32)
        nc.scalar.activation(out=hsc4[:], in_=hsc_sb[:].unsqueeze(1).unsqueeze(3).to_broadcast([P, RUNS, PACK, RUN]),
                             func=ACT.Identity, scale=4.0)
        th_cap = tile("th_cap", [P, 1], F32)
        nc.scalar.activation(out=th_cap[:], in_=th_sb[:], func=ACT.Identity, bias=CAP)
        neg_th = tile("neg_th", [P, 1], F32)
        nc.scalar.activation(out=neg_th[:], in_=th_sb[:], func=ACT.Identity, scale=-1.0)
        q_raw = load_rows("q_raw", query, Q, "hsc_sb")
        keys_pool = load_words("keys_pool", keys_words, "th_sb")

        ident = tile("ident", [P, P], F32)
        make_identity(nc, ident[:])
        scattered = tile("scattered", [P, T], F32)
        nc.vector.memset(scattered[:], 0.0)
        keys_pool_scales = load_scales("keys_pool_scales", keys_scales)

        tab_scales_g = gather("tab_scales_g", tab_pool_scales, offsets[:], SLOTS, U8)
        g_raw = load_rows("g_raw", gout, Q, "tab_pool_scales")
        w_grouped = tile("w_grouped", [P, PACK, P, PACK], BF16)
        nc.vector.tensor_copy(out=w_grouped[:].rearrange("p t m j -> p m j t"),
                              in_=w_raw[:].rearrange("p j (m t) -> p m j t", t=PACK))
        old_sb = tile("old_sb", [P, T], F32, "w_raw")
        nc.sync.dma_start(out=old_sb[:], in_=old)
        w_codes, w_scales = quantize("w", w_grouped[:].rearrange("p t m j -> p (t m j)"), R)
        reserve_sb = load_column("reserve_sb", reserve, 1, "w_grouped")

        cols = HALF // 16
        ht = []
        for h in range(HALVES):
            tab_g = gather(f"tab_g{h}", tab_pool, offsets[:, h * cols : (h + 1) * cols], HALF, U32)
            ht.append(tile(f"ht{h}", [P, GROUP, RUNS, PACK, RUN], F32))
            for pair in range(2):
                zh = ps.tile([P, 2, HALF], F32, name=f"zh{h}{pair}")
                for u in range(2):
                    t = 2 * pair + u
                    mx_product(zh[:, u, :], w_codes[:, t * P : (t + 1) * P], w_scales[:, t * P : (t + 1) * P],
                               tab_g[:], tab_scales_g[:, h * HALF : (h + 1) * HALF])
                for u in range(2):
                    t = 2 * pair + u
                    nc.scalar.activation(out=ht[h][:, :, :, t, :],
                                         in_=zh[:, u, :].rearrange("p (b i j) -> p j b i", i=RUN, j=GROUP),
                                         func=ACT.Exp, scale=temper_sb[:, t : t + 1])

        sums = []
        for h in range(HALVES):
            turn = ps.tile([P, 2, P], F32, name=f"turn{h}")
            for j in range(GROUP):
                nc.tensor.matmul(out=turn[:, 0, :], lhsT=ht[h][:, j].rearrange("p b t i -> p (b t i)"), rhs=ident[:],
                                 is_transpose=True, start=(j == 0), stop=(j == GROUP - 1))
            sums.append(turn)

        q_codes, q_scales = quantize("q", interleave_rows("q_grouped", q_raw, nc.vector.tensor_copy), Q)
        keys_scales_g = gather("keys_scales_g", keys_pool_scales, offsets[:], SLOTS, U8, "tab_pool")
        stats = tile("stats", [P, 8], F32)
        below = tile("below", [P, HALVES, GROUP, HALF // GROUP], F32)
        capped = tile("capped", [P, SLOTS], F32)
        a = []
        for h in range(HALVES):
            part = slice(h * HALF, (h + 1) * HALF)
            keys_g = gather(f"keys_g{h}", keys_pool, offsets[:, h * cols : (h + 1) * cols], HALF, U32)
            a.append(ps.tile([P, HALF], F32, name=f"a{h}"))
            mx_product(a[h][:], q_codes[:], q_scales[:], keys_g[:], keys_scales_g[:, part])
            nc.scalar.activation(out=below[:, h], in_=a[h][:].rearrange("p (g j) -> p j g", j=GROUP), func=ACT.Relu,
                                 bias=th_cap[:], scale=-1.0)
            nc.scalar.activation(out=capped[:, part], in_=below[:, h].rearrange("p j g -> p (j g)"), func=ACT.Exp,
                                 bias=CAP, scale=-1.0)
        soft = tile("soft", [P, SLOTS], F32)
        nc.scalar.activation(out=soft[:], in_=capped[:], func=ACT.Ln, bias=1.0)
        g_grouped = interleave_rows("g_grouped", g_raw, nc.scalar.copy, "capped")

        factor = []
        inv_turned = tile("inv_turned", [P, HALVES, P], F32, "th_sb")
        for h in range(HALVES):
            nc.vector.reciprocal(out=inv_turned[:, h, :], in_=sums[h][:, 0, :])
            nc.tensor.transpose(sums[h][:, 1, :], inv_turned[:, h, :], ident[:])
        hs = []
        for h in range(HALVES):
            fac = tile(f"factor{h}", [P, P], F32)
            nc.vector.tensor_tensor(out=fac[:], in0=sums[h][:, 1, :], in1=hsc4[:].rearrange("p b t i -> p (b t i)"), op=ALU.mult)
            factor.append(fac)
        def normalise(h):
            hs.append(tile(f"hs{h}", [P, GROUP, RUNS, RUN, PACK], BF16, "soft" if h == 1 else None))
            nc.vector.tensor_tensor(
                out=hs[h][:].rearrange("p j b i t -> p j b t i"), in0=ht[h][:],
                in1=factor[h][:].rearrange("p (b t i) -> p b t i", t=PACK, i=RUN).unsqueeze(1).to_broadcast([P, GROUP, RUNS, PACK, RUN]),
                op=ALU.mult)

        normalise(0)
        p_sb = tile("p_sb", [P, SLOTS], F32, "ht0")
        for h in range(HALVES):
            part = slice(h * HALF, (h + 1) * HALF)
            nc.vector.scalar_tensor_tensor(out=p_sb[:, part].rearrange("p (j g) -> p j g", j=GROUP),
                                           in0=a[h][:].rearrange("p (g j) -> p j g", j=GROUP), scalar=neg_th[:],
                                           in1=soft[:, part].rearrange("p (j g) -> p j g", j=GROUP),
                                           op0=ALU.add, op1=ALU.max, accum_out=stats[:, h : h + 1])
        sig = tile("sig", [P, SLOTS], F32)
        for h in range(HALVES):
            nc.scalar.activation(out=sig[:, h * HALF : (h + 1) * HALF], in_=a[h][:], func=ACT.Sigmoid, bias=neg_th[:])
        nc.vector.tensor_scalar(out=stats[:, 2:3], in0=stats[:, 0:1], scalar1=stats[:, 1:2], scalar2=reserve_sb[:],
                                op0=ALU.add, op1=ALU.add)
        nc.vector.reciprocal(out=stats[:, 4:5], in_=stats[:, 2:3])
        nc.vector.tensor_scalar(out=stats[:, 3:4], in0=stats[:, 4:5], scalar1=512.0, scalar2=None, op0=ALU.mult)
        nc.vector.tensor_scalar(out=stats[:, 5:6], in0=stats[:, 4:5], scalar1=stats[:, 4:5], scalar2=512.0,
                                op0=ALU.mult, op1=ALU.mult)
        g_codes, g_scales = quantize("g", g_grouped, Q)
        c0 = []

        def read_gradient(h):
            hs_codes, hs_scales = quantize(f"hs{h}", hs[h][:].rearrange("p j b i t -> p (j b i t)"), HALF)
            c0.append(ps.tile([P, HALF], F32, name=f"c0{h}", tag=f"zh0{h}"))
            mx_product(c0[h][:], g_codes[:], g_scales[:], hs_codes[:], hs_scales[:])

        read_gradient(0)
        normalise(1)
        read_gradient(1)
        weighted = tile("weighted", [P, SLOTS], F32)
        scaled = tile("scaled", [P, HALVES, HALF // GROUP, GROUP], F32)
        for h in range(HALVES):
            part = slice(h * HALF, (h + 1) * HALF)
            nc.vector.scalar_tensor_tensor(out=weighted[:, part], in0=c0[h][:], scalar=stats[:, 5:6], in1=p_sb[:, part],
                                           op0=ALU.mult, op1=ALU.mult, accum_out=stats[:, 6 + h : 7 + h])
            nc.scalar.activation(out=scaled[:, h], in_=c0[h][:].rearrange("p (j g) -> p g j", j=GROUP), func=ACT.Identity,
                                 scale=stats[:, 3:4])
        dp = tile("dp", [P, SLOTS], F32)
        for h in range(HALVES):
            part = slice(h * HALF, (h + 1) * HALF)
            nc.vector.tensor_scalar(out=dp[:, part], in0=scaled[:, h].rearrange("p g j -> p (g j)"), scalar1=stats[:, 6:7],
                                    scalar2=stats[:, 7:8], op0=ALU.subtract, op1=ALU.subtract)
            nc.vector.tensor_tensor(out=scattered[:].indirect(offsets[:, h * cols : (h + 1) * cols]), in0=dp[:, part],
                                    in1=sig[:, part], op=ALU.mult)
        for c, (lo, hi) in enumerate(zip(OUT_EDGES, OUT_EDGES[1:])):
            part = slice(lo, hi)
            res = tile(f"res{c}", [P, hi - lo], F32)
            nc.vector.tensor_tensor(out=res[:], in0=old_sb[:, part], in1=scattered[:, part], op=ALU.add)
            nc.sync.dma_start(out=out[:, part], in_=res[:])
